import numpy as np
import ml_dtypes


def mxq(x, axis, fmt="e4m3"):
    dtype, down = {"e4m3": (ml_dtypes.float8_e4m3fn, 7), "e5m2": (ml_dtypes.float8_e5m2, 14)}[fmt]
    v = np.moveaxis(np.asarray(x, np.float32).astype(ml_dtypes.bfloat16).astype(np.float64), axis, -1)
    blocks = v.reshape(v.shape[:-1] + (-1, 32))
    amax = np.abs(blocks).max(-1, keepdims=True)
    byte = np.maximum(np.where(amax > 0, np.frexp(amax)[1] - 1 + 127, 0) - down, 1)
    scale = np.exp2(byte - 127.0)
    codes = (blocks / scale).astype(np.float32).astype(dtype).astype(np.float64)
    return np.moveaxis((codes * scale).reshape(v.shape), -1, axis)


WIDE = False


def mx_kscale(k):
    if not WIDE:
        return np.ones(k)
    levels = np.array([10, -10, 5, -5, 0])
    if k % 512:
        return np.exp2(np.random.permutation(np.resize(levels, k // 32))).repeat(32)
    a = np.empty((k // 512, 16))
    for p in range(k // 512):
        a[p, :8] = np.random.permutation(np.resize(levels, 8))
        for g in range(8):
            far = levels[np.abs(levels - a[p, g]) >= 10]
            a[p, g + 8] = far[np.random.randint(len(far))]
    return np.exp2(a.ravel()).repeat(32)


def f64(x):
    return np.asarray(x).astype(np.float64)


def striped(idx):
    return np.tile(idx.reshape(-1, 16).T, (8, 1)).astype(np.uint16)


def unstriped(offs):
    return offs[:16].T.reshape(-1).astype(np.int64)


def pack_weight(w):
    k, n = w.shape
    w = f64(np.asarray(w, np.float32).astype(ml_dtypes.bfloat16)).reshape(k // 32, 32, n)
    amax = np.abs(w).max(1)
    byte = np.clip(np.where(amax > 0, np.frexp(amax)[1] - 1 + 127 - 7, 1), 1, 254)
    scaled = (w * np.exp2(127.0 - byte)[:, None, :]).reshape(k, n).astype(np.float32)
    words = np.ascontiguousarray(scaled.reshape(k // 512, 128, 4, n).transpose(0, 1, 3, 2)).astype(ml_dtypes.float8_e4m3fn).view(np.uint8)
    return words, np.ascontiguousarray(byte.astype(np.uint8).reshape(k // 512, 16, n))


def unpack_weight(words, scales):
    g, p, n, _ = words.shape
    vals = np.ascontiguousarray(words).view(ml_dtypes.float8_e4m3fn).astype(np.float64) * np.repeat(np.exp2(scales.astype(np.float64) - 127.0), 8, axis=1)[..., None]
    return vals.transpose(0, 1, 3, 2).reshape(g * 512, n)


def relu(v):
    return np.maximum(v, 0.0)


def sigmoid(v):
    return 1.0 / (1.0 + np.exp(-np.maximum(v, -700.0)))


K, T, S, D, N, V = 512, 2048, 1024, 4, 256, 256
P = 2 ** 7


def setup_inputs():
    n = np.random.standard_normal
    s = mx_kscale(K)[:, None]
    packed_xT = pack_weight(n((K, T)) * s)
    return {
        "x_words": packed_xT[0],
        "x_scales": packed_xT[1],
        "w1": (n((K, N)) / np.sqrt(K) / s).astype(np.float32),
        "thr": (np.tile(-np.random.uniform(0.2, 1.5, S), (P, 1))).astype(np.float32),
        "mkt": (0.5 * n((N, 1))).astype(np.float32),
        "lgd": (np.tile(np.random.uniform(0.3, 1.0, S), (P, 1))).astype(np.float32),
        "att": (np.tile(np.random.uniform(0.1, 0.4, V) * D, (P, 1))).astype(np.float32),
        "wid": (np.tile(np.random.uniform(0.1, 0.3, V) * D, (P, 1))).astype(np.float32),
        "offs": striped(np.random.permutation(T)[:S]),
    }


def reference(x_words, x_scales, w1, thr, mkt, lgd, att, wid, offs):
    xq = unpack_weight(x_words, x_scales)[:, unstriped(offs)]
    y = mxq(f64(w1), 0, "e4m3").T @ xq
    pd = sigmoid(1.7 * (f64(thr)[:1] - (0.7 * y) + f64(mkt)))
    el = pd * f64(lgd)[:1]
    loss = el.reshape(len(el), -1, D).sum(axis=2)
    return np.minimum(relu(loss - f64(att)[:1]), f64(wid)[:1])

@@ -1,0 +1,168 @@
+from contextlib import ExitStack
+
+import concourse.mybir as mybir
+from concourse.masks import make_identity
+
+K, T, S, D, M = 512, 2048, 1024, 4, 256
+FLOPS = 2 * K * M * S
+
+F32 = mybir.dt.float32
+BF16 = mybir.dt.bfloat16
+I32 = mybir.dt.int32
+U32 = mybir.dt.uint32
+U16 = mybir.dt.uint16
+U8 = mybir.dt.uint8
+FP8X4 = mybir.dt.float8_e4m3fn_x4
+ALU = mybir.AluOpType
+ACT = mybir.ActivationFunctionType
+
+P = 128
+PACK = 4
+HALVES = S // (D * P)
+HALF = D * P
+LIST_COLS = HALF // 16
+ROW_BLOCKS = M // P
+
+
+def tile_picked_ytranch_cut_p_kernel(tc, x_words, x_scales, w1, thr, mkt, lgd, att, wid, offs, out):
+    nc = tc.nc
+    with ExitStack() as ctx:
+        sb = ctx.enter_context(tc.tile_pool(name="sb", bufs=1))
+        ps = ctx.enter_context(tc.psum_pool(name="ps", bufs=1))
+
+        offsets = sb.tile([P, S // 16], U16, name="offsets")
+        nc.sync.dma_start(offsets[:], offs)
+        mkt_col = sb.tile([P, ROW_BLOCKS], F32, name="mkt_col")
+        with nc.allow_non_contiguous_dma(reason="one value a partition"):
+            nc.sync.dma_start(mkt_col[:], mkt.rearrange("(h p) o -> p (h o)", p=P))
+
+        scale_table = sb.tile([P, T], U8, name="scale_table", align_bytes=64)
+        nc.vector.memset(scale_table[:].bitcast(I32), 0)
+        for q in range(4):
+            nc.sync.dma_start(
+                scale_table[32 * q : 32 * q + 4, :].bitcast(I32),
+                x_scales[0, 4 * q : 4 * q + 4, :].bitcast(I32),
+            )
+
+        w_raw = sb.tile([P, PACK, M], F32, name="w_raw")
+        nc.sync.dma_start(w_raw[:], w1.rearrange("(p t) m -> p t m", t=PACK))
+        word_table = sb.tile([P, T], I32, name="word_table", align_bytes=64)
+        nc.sync.dma_start(word_table[:], x_words[0].rearrange("p c t -> p (c t)").bitcast(I32))
+
+        thr_col = sb.tile([P, HALVES, D], F32, name="thr_col")
+        lgd_col = sb.tile([P, HALVES, D], F32, name="lgd_col")
+        att_col = sb.tile([P, HALVES], F32, name="att_col")
+        with nc.allow_non_contiguous_dma(reason="one value a partition"):
+            nc.sync.dma_start(thr_col[:], thr[0].rearrange("(b p d) -> p b d", p=P, d=D))
+            nc.sync.dma_start(lgd_col[:], lgd[0].rearrange("(b p d) -> p b d", p=P, d=D))
+            nc.sync.dma_start(att_col[:], att[0].rearrange("(b p) -> p b", p=P))
+        wid_rows = sb.tile([P, M], F32, name="wid_rows")
+        nc.sync.dma_start(wid_rows[:], wid)
+
+        identity = sb.tile([P, P], F32, name="identity")
+        make_identity(nc, identity[:])
+
+        picked_scales = []
+        dealt_scales = []
+        for b in range(HALVES):
+            picked = sb.tile([P, HALF], U8, name=f"picked_scales{b}", align_bytes=64)
+            nc.vector.tensor_copy(
+                picked[:], scale_table[:].indirect(offsets[:, b * LIST_COLS : (b + 1) * LIST_COLS])
+            )
+            picked_scales.append(picked)
+        for b in range(HALVES):
+            dealt = sb.tile([P, D, P], U8, name=f"dealt_scales{b}", align_bytes=64)
+            nc.vector.tensor_copy(dealt[:], picked_scales[b][:].rearrange("p (v d) -> p d v", d=D))
+            dealt_scales.append(dealt)
+
+        w_grouped = sb.tile([P, M, PACK], BF16, name="w_grouped", align_bytes=64)
+        nc.scalar.activation(w_grouped[:], w_raw[:].rearrange("p t m -> p m t"), ACT.Copy)
+        w_words = sb.tile([P, M], U32, name="w_words", align_bytes=64)
+        w_scales = sb.tile([P, M], U8, name="w_scales", align_bytes=64)
+        nc.vector.quantize_mx(
+            out=w_words[:].bitcast(FP8X4),
+            scales=w_scales[:],
+            in_=w_grouped[:].rearrange("p m t -> p (m t)"),
+        )
+
+        mkt_bank = ps.tile([P, M], F32, name="mkt_bank", tag="sum0")
+        for h in range(ROW_BLOCKS):
+            nc.tensor.transpose(
+                mkt_bank[:, h * P : (h + 1) * P], mkt_col[:, h : h + 1].to_broadcast([P, P]), identity[:]
+            )
+        mkt_rows = sb.tile([P, M], F32, name="mkt_rows")
+        nc.scalar.copy(mkt_rows[:], mkt_bank[:])
+
+        thr_bias = sb.tile([P, HALVES, D], F32, name="thr_bias")
+        nc.scalar.activation(thr_bias[:], thr_col[:], ACT.Copy, scale=0.85)
+        half_lgd = sb.tile([P, HALVES, D], F32, name="half_lgd")
+        nc.scalar.activation(half_lgd[:], lgd_col[:], ACT.Copy, scale=0.5)
+        first_addend = sb.tile([P, HALVES], F32, name="first_addend")
+        for b in range(HALVES):
+            nc.scalar.activation(
+                first_addend[:, b : b + 1], att_col[:, b : b + 1], ACT.Identity,
+                bias=half_lgd[:, b, 0:1], scale=-1.0,
+            )
+
+        dealt_words = []
+        for b in range(HALVES):
+            dealt = sb.tile([P, D, P], U32, name=f"dealt_words{b}", align_bytes=64)
+            nc.vector.tensor_copy(
+                dealt[:].rearrange("p d v -> p v d"),
+                word_table[:].bitcast(U32).indirect(offsets[:, b * LIST_COLS : (b + 1) * LIST_COLS]),
+            )
+            dealt_words.append(dealt)
+
+        groups = [[(0, 1), (2, 3)], [(0,), (1,), (2,), (3,)]]
+        y_tags = [["pair0", "pair1"], ["one0", "one1", "one2", "one3"]]
+        sum_tags = [["sum0", "sum1"], ["pair0", "pair1"]]
+        y_banks = {}
+        for b in range(HALVES):
+            for g, members in enumerate(groups[b]):
+                bank = ps.tile([P, len(members), M], F32, name=f"y{b}_{g}", tag=y_tags[b][g])
+                for i, d in enumerate(members):
+                    nc.tensor.matmul_mx(
+                        out=bank[:, i, :],
+                        lhsT=dealt_words[b][:, d, :].bitcast(FP8X4),
+                        lhsT_scale=dealt_scales[b][:, d, :],
+                        rhs=w_words[:].bitcast(FP8X4),
+                        rhs_scale=w_scales[:],
+                        start=True,
+                        stop=True,
+                    )
+                y_banks[(b, g)] = bank
+
+        tanhs = {}
+        for b in range(HALVES):
+            for g, members in enumerate(groups[b]):
+                n = len(members)
+                z = sb.tile([P, n, M], F32, name=f"z{b}_{g}")
+                nc.vector.scalar_tensor_tensor(
+                    z[:], y_banks[(b, g)][:], -0.7,
+                    mkt_rows[:].unsqueeze(1).to_broadcast([P, n, M]), ALU.mult, ALU.add,
+                )
+                for i, d in enumerate(members):
+                    t = sb.tile([P, M], F32, name=f"tanh{b}_{d}")
+                    nc.scalar.activation(t[:], z[:, i, :], ACT.Tanh, bias=thr_bias[:, b, d : d + 1], scale=0.85)
+                    tanhs[(b, d)] = t
+
+        for b in range(HALVES):
+            sums = [ps.tile([P, P], F32, name=f"sum{b}_{h}", tag=sum_tags[b][h]) for h in range(ROW_BLOCKS)]
+            for d in range(D):
+                el = sb.tile([P, M], F32, name=f"el{b}_{d}")
+                addend = first_addend[:, b : b + 1] if d == 0 else half_lgd[:, b, d : d + 1]
+                engine = nc.gpsimd if b == 0 else nc.vector
+                engine.tensor_scalar(el[:], tanhs[(b, d)][:], half_lgd[:, b, d : d + 1], addend, ALU.mult, ALU.add)
+                for h in range(ROW_BLOCKS):
+                    nc.tensor.matmul(
+                        sums[h][:], el[:, h * P : (h + 1) * P], identity[:],
+                        is_transpose=True, start=(d == 0), stop=(d == D - 1),
+                    )
+            result = sb.tile([P, ROW_BLOCKS, P], F32, name=f"result{b}")
+            for h in range(ROW_BLOCKS):
+                nc.vector.scalar_tensor_tensor(
+                    result[:, h, :], sums[h][:], 0.0, wid_rows[:, b * P : (b + 1) * P], ALU.max, ALU.min
+                )
+            nc.sync.dma_start(
+                out[:, b * P : (b + 1) * P].rearrange("(h p) v -> p h v", p=P), result[:]
+            )

@@ -22,45 +22,39 @@ HALVES = S // (D * P)
 HALF = D * P
 LIST_COLS = HALF // 16
 ROW_BLOCKS = M // P
+WORDS_BYTES = 4 * HALF
 
 
 def tile_picked_ytranch_cut_p_kernel(tc, x_words, x_scales, w1, thr, mkt, lgd, att, wid, offs, out):
     nc = tc.nc
     with ExitStack() as ctx:
         sb = ctx.enter_context(tc.tile_pool(name="sb", bufs=1))
+        shared = ctx.enter_context(tc.tile_pool(name="shared", bufs=1))
         ps = ctx.enter_context(tc.psum_pool(name="ps", bufs=1))
 
         offsets = sb.tile([P, S // 16], U16, name="offsets")
         nc.sync.dma_start(offsets[:], offs)
-        mkt_col = sb.tile([P, ROW_BLOCKS], F32, name="mkt_col")
+        mkt_col = sb.tile([P, ROW_BLOCKS], F32, name="mkt_col", tag="columns")
         with nc.allow_non_contiguous_dma(reason="one value a partition"):
             nc.sync.dma_start(mkt_col[:], mkt.rearrange("(h p) o -> p (h o)", p=P))
 
         scale_table = sb.tile([P, T], U8, name="scale_table", align_bytes=64)
         nc.vector.memset(scale_table[:].bitcast(I32), 0)
-        for q in range(4):
-            nc.sync.dma_start(
-                scale_table[32 * q : 32 * q + 4, :].bitcast(I32),
-                x_scales[0, 4 * q : 4 * q + 4, :].bitcast(I32),
-            )
+        for r in range(4):
+            queue = nc.sync if r % 2 == 0 else nc.scalar
+            queue.dma_start(scale_table[r:P:32, :].bitcast(I32), x_scales[0, r:16:4, :].bitcast(I32))
 
         w_raw = sb.tile([P, PACK, M], F32, name="w_raw")
         nc.sync.dma_start(w_raw[:], w1.rearrange("(p t) m -> p t m", t=PACK))
         word_table = sb.tile([P, T], I32, name="word_table", align_bytes=64)
         nc.sync.dma_start(word_table[:], x_words[0].rearrange("p c t -> p (c t)").bitcast(I32))
 
-        thr_col = sb.tile([P, HALVES, D], F32, name="thr_col")
-        lgd_col = sb.tile([P, HALVES, D], F32, name="lgd_col")
-        att_col = sb.tile([P, HALVES], F32, name="att_col")
-        with nc.allow_non_contiguous_dma(reason="one value a partition"):
-            nc.sync.dma_start(thr_col[:], thr[0].rearrange("(b p d) -> p b d", p=P, d=D))
-            nc.sync.dma_start(lgd_col[:], lgd[0].rearrange("(b p d) -> p b d", p=P, d=D))
-            nc.sync.dma_start(att_col[:], att[0].rearrange("(b p) -> p b", p=P))
         wid_rows = sb.tile([P, M], F32, name="wid_rows")
         nc.sync.dma_start(wid_rows[:], wid)
 
         identity = sb.tile([P, P], F32, name="identity")
-        make_identity(nc, identity[:])
+        nc.vector.memset(identity[:], 0.0)
+        make_identity(nc, identity[:], nomemset=True)
 
         picked_scales = []
         dealt_scales = []
@@ -75,7 +69,7 @@ def tile_picked_ytranch_cut_p_kernel(tc, x_words, x_scales, w1, thr, mkt, lgd, a
             nc.vector.tensor_copy(dealt[:], picked_scales[b][:].rearrange("p (v d) -> p d v", d=D))
             dealt_scales.append(dealt)
 
-        w_grouped = sb.tile([P, M, PACK], BF16, name="w_grouped", align_bytes=64)
+        w_grouped = shared.tile([P, M, PACK], BF16, name="w_grouped", offset=WORDS_BYTES // 2, align_bytes=64)
         nc.scalar.activation(w_grouped[:], w_raw[:].rearrange("p t m -> p m t"), ACT.Copy)
         w_words = sb.tile([P, M], U32, name="w_words", align_bytes=64)
         w_scales = sb.tile([P, M], U8, name="w_scales", align_bytes=64)
@@ -85,84 +79,116 @@ def tile_picked_ytranch_cut_p_kernel(tc, x_words, x_scales, w1, thr, mkt, lgd, a
             in_=w_grouped[:].rearrange("p m t -> p (m t)"),
         )
 
-        mkt_bank = ps.tile([P, M], F32, name="mkt_bank", tag="sum0")
+        mkt_bank = ps.tile([P, M], F32, name="mkt_bank", tag="sum1_1")
         for h in range(ROW_BLOCKS):
             nc.tensor.transpose(
                 mkt_bank[:, h * P : (h + 1) * P], mkt_col[:, h : h + 1].to_broadcast([P, P]), identity[:]
             )
         mkt_rows = sb.tile([P, M], F32, name="mkt_rows")
-        nc.scalar.copy(mkt_rows[:], mkt_bank[:])
+        nc.scalar.activation(mkt_rows[:], mkt_bank[:], ACT.Copy)
+
+        columns = sb.tile([P, 3, HALVES, D], F32, name="columns", tag="columns")
+        thr_col = columns[:, 0]
+        lgd_col = columns[:, 1]
+        att_col = columns[:, 2, 0, 0:HALVES]
+        with nc.allow_non_contiguous_dma(reason="one value a partition"):
+            nc.scalar.dma_start(thr_col, thr[0].rearrange("(b p d) -> p b d", p=P, d=D))
+            nc.scalar.dma_start(lgd_col, lgd[0].rearrange("(b p d) -> p b d", p=P, d=D))
+            nc.scalar.dma_start(att_col, att[0].rearrange("(b p) -> p b", p=P))
 
         thr_bias = sb.tile([P, HALVES, D], F32, name="thr_bias")
-        nc.scalar.activation(thr_bias[:], thr_col[:], ACT.Copy, scale=0.85)
+        nc.scalar.activation(thr_bias[:], thr_col, ACT.Copy, scale=0.85)
         half_lgd = sb.tile([P, HALVES, D], F32, name="half_lgd")
-        nc.scalar.activation(half_lgd[:], lgd_col[:], ACT.Copy, scale=0.5)
-        first_addend = sb.tile([P, HALVES], F32, name="first_addend")
+        half_sum = sb.tile([P, HALVES], F32, name="half_sum")
+        constant = sb.tile([P, HALVES], F32, name="constant")
         for b in range(HALVES):
             nc.scalar.activation(
-                first_addend[:, b : b + 1], att_col[:, b : b + 1], ACT.Identity,
-                bias=half_lgd[:, b, 0:1], scale=-1.0,
+                half_lgd[:, b, :], lgd_col[:, b, :], ACT.Identity, scale=0.5, accum_out=half_sum[:, b : b + 1]
+            )
+            nc.scalar.activation(
+                constant[:, b : b + 1], att_col[:, b : b + 1], ACT.Identity,
+                bias=half_sum[:, b : b + 1], scale=-1.0,
             )
 
         dealt_words = []
         for b in range(HALVES):
-            dealt = sb.tile([P, D, P], U32, name=f"dealt_words{b}", align_bytes=64)
+            dealt = shared.tile([P, D, P], U32, name=f"dealt_words{b}", offset=b * WORDS_BYTES, align_bytes=64)
             nc.vector.tensor_copy(
                 dealt[:].rearrange("p d v -> p v d"),
                 word_table[:].bitcast(U32).indirect(offsets[:, b * LIST_COLS : (b + 1) * LIST_COLS]),
             )
             dealt_words.append(dealt)
 
-        groups = [[(0, 1), (2, 3)], [(0,), (1,), (2,), (3,)]]
-        y_tags = [["pair0", "pair1"], ["one0", "one1", "one2", "one3"]]
-        sum_tags = [["sum0", "sum1"], ["pair0", "pair1"]]
-        y_banks = {}
-        for b in range(HALVES):
-            for g, members in enumerate(groups[b]):
-                bank = ps.tile([P, len(members), M], F32, name=f"y{b}_{g}", tag=y_tags[b][g])
-                for i, d in enumerate(members):
-                    nc.tensor.matmul_mx(
-                        out=bank[:, i, :],
-                        lhsT=dealt_words[b][:, d, :].bitcast(FP8X4),
-                        lhsT_scale=dealt_scales[b][:, d, :],
-                        rhs=w_words[:].bitcast(FP8X4),
-                        rhs_scale=w_scales[:],
-                        start=True,
-                        stop=True,
-                    )
-                y_banks[(b, g)] = bank
-
-        tanhs = {}
-        for b in range(HALVES):
-            for g, members in enumerate(groups[b]):
-                n = len(members)
-                z = sb.tile([P, n, M], F32, name=f"z{b}_{g}")
-                nc.vector.scalar_tensor_tensor(
-                    z[:], y_banks[(b, g)][:], -0.7,
-                    mkt_rows[:].unsqueeze(1).to_broadcast([P, n, M]), ALU.mult, ALU.add,
+        steps = [(b, d) for b in range(HALVES) for d in range(D)]
+        PAIR = 2
+        tanhs = []
+        sums = {}
+        for pair in range(len(steps) // PAIR):
+            members = steps[PAIR * pair : PAIR * (pair + 1)]
+            bank = ps.tile([P, PAIR, M], F32, name=f"y{pair}")
+            for i, (b, d) in enumerate(members):
+                nc.tensor.matmul_mx(
+                    out=bank[:, i, :],
+                    lhsT=dealt_words[b][:, d, :].bitcast(FP8X4),
+                    lhsT_scale=dealt_scales[b][:, d, :],
+                    rhs=w_words[:].bitcast(FP8X4),
+                    rhs_scale=w_scales[:],
+                    start=True,
+                    stop=True,
                 )
-                for i, d in enumerate(members):
-                    t = sb.tile([P, M], F32, name=f"tanh{b}_{d}")
-                    nc.scalar.activation(t[:], z[:, i, :], ACT.Tanh, bias=thr_bias[:, b, d : d + 1], scale=0.85)
-                    tanhs[(b, d)] = t
-
-        for b in range(HALVES):
-            sums = [ps.tile([P, P], F32, name=f"sum{b}_{h}", tag=sum_tags[b][h]) for h in range(ROW_BLOCKS)]
-            for d in range(D):
-                el = sb.tile([P, M], F32, name=f"el{b}_{d}")
-                addend = first_addend[:, b : b + 1] if d == 0 else half_lgd[:, b, d : d + 1]
-                engine = nc.gpsimd if b == 0 else nc.vector
-                engine.tensor_scalar(el[:], tanhs[(b, d)][:], half_lgd[:, b, d : d + 1], addend, ALU.mult, ALU.add)
-                for h in range(ROW_BLOCKS):
-                    nc.tensor.matmul(
-                        sums[h][:], el[:, h * P : (h + 1) * P], identity[:],
-                        is_transpose=True, start=(d == 0), stop=(d == D - 1),
-                    )
-            result = sb.tile([P, ROW_BLOCKS, P], F32, name=f"result{b}")
-            for h in range(ROW_BLOCKS):
-                nc.vector.scalar_tensor_tensor(
-                    result[:, h, :], sums[h][:], 0.0, wid_rows[:, b * P : (b + 1) * P], ALU.max, ALU.min
-                )
-            nc.sync.dma_start(
-                out[:, b * P : (b + 1) * P].rearrange("(h p) v -> p h v", p=P), result[:]
+            z = sb.tile([P, PAIR, M], F32, name=f"z{pair}")
+            nc.vector.scalar_tensor_tensor(
+                z[:], bank[:], -0.7, mkt_rows[:].unsqueeze(1).to_broadcast([P, PAIR, M]), ALU.mult, ALU.add
             )
+            for i, (b, d) in enumerate(members):
+                t = sb.tile([P, M], F32, name=f"tanh{b}_{d}")
+                nc.scalar.activation(t[:], z[:, i, :], ACT.Tanh, bias=thr_bias[:, b, d : d + 1], scale=0.85)
+                tanhs.append(t)
+
+        evens = {}
+
+        def weigh_even(pair):
+            b, d = steps[PAIR * pair]
+            el = sb.tile([P, M], F32, name=f"even{pair}")
+            factor = half_lgd[:, b, d : d + 1]
+            addend = constant[:, b : b + 1] if d == 0 else 0.0
+            if pair == 3:
+                nc.scalar.activation(el[:], tanhs[PAIR * pair][:], ACT.Copy, scale=factor)
+            else:
+                engine = nc.gpsimd if b == 0 else nc.vector
+                engine.tensor_scalar(el[:], tanhs[PAIR * pair][:], factor, addend, ALU.mult, ALU.add)
+            evens[pair] = el
+
+        def weigh_odd_and_sum(pair):
+            b, d = steps[PAIR * pair + 1]
+            el = sb.tile([P, M], F32, name=f"both{pair}")
+            nc.vector.scalar_tensor_tensor(
+                el[:], tanhs[PAIR * pair + 1][:], half_lgd[:, b, d : d + 1], evens[pair][:], ALU.mult, ALU.add
+            )
+            for h in range(ROW_BLOCKS):
+                if d == 1:
+                    sums[(b, h)] = ps.tile([P, P], F32, name=f"sum{b}_{h}", tag=f"sum{b}_{h}")
+                nc.tensor.matmul(
+                    sums[(b, h)][:], el[:, h * P : (h + 1) * P], identity[:],
+                    is_transpose=True, start=(d == 1), stop=(d == D - 1),
+                )
+
+        def clamp_and_store(b):
+            for h in range(ROW_BLOCKS):
+                result = sb.tile([P, P], F32, name=f"result{b}_{h}")
+                nc.vector.scalar_tensor_tensor(
+                    result[:], sums[(b, h)][:], 0.0, wid_rows[:, b * P : (b + 1) * P], ALU.max, ALU.min
+                )
+                queue = nc.sync if h == 0 else nc.scalar
+                queue.dma_start(out[h * P : (h + 1) * P, b * P : (b + 1) * P], result[:])
+
+        weigh_even(0)
+        weigh_even(1)
+        weigh_odd_and_sum(0)
+        weigh_even(2)
+        weigh_odd_and_sum(1)
+        weigh_even(3)
+        weigh_odd_and_sum(2)
+        weigh_odd_and_sum(3)
+        clamp_and_store(0)
+        clamp_and_store(1)

@@ -34,9 +34,8 @@ def tile_picked_ytranch_cut_p_kernel(tc, x_words, x_scales, w1, thr, mkt, lgd, a
 
         offsets = sb.tile([P, S // 16], U16, name="offsets")
         nc.sync.dma_start(offsets[:], offs)
-        mkt_col = sb.tile([P, ROW_BLOCKS], F32, name="mkt_col", tag="columns")
-        with nc.allow_non_contiguous_dma(reason="one value a partition"):
-            nc.sync.dma_start(mkt_col[:], mkt.rearrange("(h p) o -> p (h o)", p=P))
+        wid_rows = sb.tile([P, M], F32, name="wid_rows")
+        nc.sync.dma_start(wid_rows[:], wid)
 
         scale_table = sb.tile([P, T], U8, name="scale_table", align_bytes=64)
         nc.vector.memset(scale_table[:].bitcast(I32), 0)
@@ -49,8 +48,15 @@ def tile_picked_ytranch_cut_p_kernel(tc, x_words, x_scales, w1, thr, mkt, lgd, a
         word_table = sb.tile([P, T], I32, name="word_table", align_bytes=64)
         nc.sync.dma_start(word_table[:], x_words[0].rearrange("p c t -> p (c t)").bitcast(I32))
 
-        wid_rows = sb.tile([P, M], F32, name="wid_rows")
-        nc.sync.dma_start(wid_rows[:], wid)
+        mkt_col = sb.tile([P, ROW_BLOCKS], F32, name="mkt_col")
+        lgd_col = sb.tile([P, HALVES, D], F32, name="lgd_col")
+        att_col = sb.tile([P, HALVES], F32, name="att_col")
+        thr_col = sb.tile([P, HALVES, D], F32, name="thr_col")
+        with nc.allow_non_contiguous_dma(reason="one value a partition"):
+            nc.sync.dma_start(mkt_col[:], mkt.rearrange("(h p) o -> p (h o)", p=P))
+            nc.sync.dma_start(lgd_col[:], lgd[0].rearrange("(b p d) -> p b d", p=P, d=D))
+            nc.sync.dma_start(att_col[:], att[0].rearrange("(b p) -> p b", p=P))
+            nc.sync.dma_start(thr_col[:], thr[0].rearrange("(b p d) -> p b d", p=P, d=D))
 
         identity = sb.tile([P, P], F32, name="identity")
         nc.vector.memset(identity[:], 0.0)
@@ -79,25 +85,14 @@ def tile_picked_ytranch_cut_p_kernel(tc, x_words, x_scales, w1, thr, mkt, lgd, a
             in_=w_grouped[:].rearrange("p m t -> p (m t)"),
         )
 
-        mkt_bank = ps.tile([P, M], F32, name="mkt_bank", tag="sum1_1")
-        for h in range(ROW_BLOCKS):
-            nc.tensor.transpose(
-                mkt_bank[:, h * P : (h + 1) * P], mkt_col[:, h : h + 1].to_broadcast([P, P]), identity[:]
-            )
         mkt_rows = sb.tile([P, M], F32, name="mkt_rows")
-        nc.scalar.activation(mkt_rows[:], mkt_bank[:], ACT.Copy)
-
-        columns = sb.tile([P, 3, HALVES, D], F32, name="columns", tag="columns")
-        thr_col = columns[:, 0]
-        lgd_col = columns[:, 1]
-        att_col = columns[:, 2, 0, 0:HALVES]
-        with nc.allow_non_contiguous_dma(reason="one value a partition"):
-            nc.scalar.dma_start(thr_col, thr[0].rearrange("(b p d) -> p b d", p=P, d=D))
-            nc.scalar.dma_start(lgd_col, lgd[0].rearrange("(b p d) -> p b d", p=P, d=D))
-            nc.scalar.dma_start(att_col, att[0].rearrange("(b p) -> p b", p=P))
+        for h in range(ROW_BLOCKS):
+            mkt_bank = ps.tile([P, P], F32, name=f"mkt_bank{h}", tag=f"y{h}")
+            nc.tensor.transpose(mkt_bank[:], mkt_col[:, h : h + 1].to_broadcast([P, P]), identity[:])
+            nc.scalar.activation(mkt_rows[:, h * P : (h + 1) * P], mkt_bank[:], ACT.Copy)
 
         thr_bias = sb.tile([P, HALVES, D], F32, name="thr_bias")
-        nc.scalar.activation(thr_bias[:], thr_col, ACT.Copy, scale=0.85)
+        nc.scalar.activation(thr_bias[:], thr_col[:], ACT.Copy, scale=0.85)
         half_lgd = sb.tile([P, HALVES, D], F32, name="half_lgd")
         half_sum = sb.tile([P, HALVES], F32, name="half_sum")
         constant = sb.tile([P, HALVES], F32, name="constant")
@@ -125,7 +120,7 @@ def tile_picked_ytranch_cut_p_kernel(tc, x_words, x_scales, w1, thr, mkt, lgd, a
         sums = {}
         for pair in range(len(steps) // PAIR):
             members = steps[PAIR * pair : PAIR * (pair + 1)]
-            bank = ps.tile([P, PAIR, M], F32, name=f"y{pair}")
+            bank = ps.tile([P, PAIR, M], F32, name=f"y{pair}", tag=f"y{pair}")
             for i, (b, d) in enumerate(members):
                 nc.tensor.matmul_mx(
                     out=bank[:, i, :],
@@ -141,7 +136,7 @@ def tile_picked_ytranch_cut_p_kernel(tc, x_words, x_scales, w1, thr, mkt, lgd, a
                 z[:], bank[:], -0.7, mkt_rows[:].unsqueeze(1).to_broadcast([P, PAIR, M]), ALU.mult, ALU.add
             )
             for i, (b, d) in enumerate(members):
-                t = sb.tile([P, M], F32, name=f"tanh{b}_{d}")
+                t = sb.tile([P, M], F32, name=f"tanh{b}_{d}", tag=f"tanh{b}_{d}")
                 nc.scalar.activation(t[:], z[:, i, :], ACT.Tanh, bias=thr_bias[:, b, d : d + 1], scale=0.85)
                 tanhs.append(t)
 
@@ -149,14 +144,13 @@ def tile_picked_ytranch_cut_p_kernel(tc, x_words, x_scales, w1, thr, mkt, lgd, a
 
         def weigh_even(pair):
             b, d = steps[PAIR * pair]
-            el = sb.tile([P, M], F32, name=f"even{pair}")
+            el = sb.tile([P, M], F32, name=f"even{pair}", tag=f"even{pair}")
             factor = half_lgd[:, b, d : d + 1]
             addend = constant[:, b : b + 1] if d == 0 else 0.0
-            if pair == 3:
-                nc.scalar.activation(el[:], tanhs[PAIR * pair][:], ACT.Copy, scale=factor)
+            if b == 0:
+                nc.gpsimd.tensor_scalar(el[:], tanhs[PAIR * pair][:], factor, addend, ALU.mult, ALU.add)
             else:
-                engine = nc.gpsimd if b == 0 else nc.vector
-                engine.tensor_scalar(el[:], tanhs[PAIR * pair][:], factor, addend, ALU.mult, ALU.add)
+                nc.scalar.activation(el[:], tanhs[PAIR * pair][:], ACT.Identity, bias=addend, scale=factor)
             evens[pair] = el
 
         def weigh_odd_and_sum(pair):
@@ -175,7 +169,8 @@ def tile_picked_ytranch_cut_p_kernel(tc, x_words, x_scales, w1, thr, mkt, lgd, a
 
         def clamp_and_store(b):
             for h in range(ROW_BLOCKS):
-                result = sb.tile([P, P], F32, name=f"result{b}_{h}")
+                tag = f"result{h}" if b == 1 else ("tanh1_3", "even3")[h]
+                result = sb.tile([P, P], F32, name=f"result{b}_{h}", tag=tag)
                 nc.vector.scalar_tensor_tensor(
                     result[:], sums[(b, h)][:], 0.0, wid_rows[:, b * P : (b + 1) * P], ALU.max, ALU.min
                 )
@@ -184,10 +179,10 @@ def tile_picked_ytranch_cut_p_kernel(tc, x_words, x_scales, w1, thr, mkt, lgd, a
 
         weigh_even(0)
         weigh_even(1)
-        weigh_odd_and_sum(0)
         weigh_even(2)
-        weigh_odd_and_sum(1)
         weigh_even(3)
+        weigh_odd_and_sum(0)
+        weigh_odd_and_sum(1)
         weigh_odd_and_sum(2)
         weigh_odd_and_sum(3)
         clamp_and_store(0)

from contextlib import ExitStack

import concourse.mybir as mybir
from concourse.masks import make_identity

K, T, S, D, M = 512, 2048, 1024, 4, 256
FLOPS = 2 * K * M * S

F32 = mybir.dt.float32
BF16 = mybir.dt.bfloat16
I32 = mybir.dt.int32
U32 = mybir.dt.uint32
U16 = mybir.dt.uint16
U8 = mybir.dt.uint8
FP8X4 = mybir.dt.float8_e4m3fn_x4
ALU = mybir.AluOpType
ACT = mybir.ActivationFunctionType

P = 128
PACK = 4
HALVES = S // (D * P)
HALF = D * P
LIST_COLS = HALF // 16
ROW_BLOCKS = M // P
WORDS_BYTES = 4 * HALF


def tile_picked_ytranch_cut_p_kernel(tc, x_words, x_scales, w1, thr, mkt, lgd, att, wid, offs, out):
    nc = tc.nc
    with ExitStack() as ctx:
        sb = ctx.enter_context(tc.tile_pool(name="sb", bufs=1))
        shared = ctx.enter_context(tc.tile_pool(name="shared", bufs=1))
        ps = ctx.enter_context(tc.psum_pool(name="ps", bufs=1))

        offsets = sb.tile([P, S // 16], U16, name="offsets")
        nc.sync.dma_start(offsets[:], offs)
        wid_rows = sb.tile([P, M], F32, name="wid_rows")
        nc.sync.dma_start(wid_rows[:], wid)

        scale_table = sb.tile([P, T], U8, name="scale_table", align_bytes=64)
        nc.vector.memset(scale_table[:].bitcast(I32), 0)
        for r in range(4):
            queue = nc.sync if r % 2 == 0 else nc.scalar
            queue.dma_start(scale_table[r:P:32, :].bitcast(I32), x_scales[0, r:16:4, :].bitcast(I32))

        w_raw = sb.tile([P, PACK, M], F32, name="w_raw")
        nc.sync.dma_start(w_raw[:], w1.rearrange("(p t) m -> p t m", t=PACK))
        word_table = sb.tile([P, T], I32, name="word_table", align_bytes=64)
        nc.sync.dma_start(word_table[:], x_words[0].rearrange("p c t -> p (c t)").bitcast(I32))

        mkt_col = sb.tile([P, ROW_BLOCKS], F32, name="mkt_col")
        lgd_col = sb.tile([P, HALVES, D], F32, name="lgd_col")
        att_col = sb.tile([P, HALVES], F32, name="att_col")
        thr_col = sb.tile([P, HALVES, D], F32, name="thr_col")
        with nc.allow_non_contiguous_dma(reason="one value a partition"):
            nc.sync.dma_start(mkt_col[:], mkt.rearrange("(h p) o -> p (h o)", p=P))
            nc.sync.dma_start(lgd_col[:], lgd[0].rearrange("(b p d) -> p b d", p=P, d=D))
            nc.sync.dma_start(att_col[:], att[0].rearrange("(b p) -> p b", p=P))
            nc.sync.dma_start(thr_col[:], thr[0].rearrange("(b p d) -> p b d", p=P, d=D))

        identity = sb.tile([P, P], F32, name="identity")
        nc.vector.memset(identity[:], 0.0)
        make_identity(nc, identity[:], nomemset=True)

        picked_scales = []
        dealt_scales = []
        for b in range(HALVES):
            picked = sb.tile([P, HALF], U8, name=f"picked_scales{b}", align_bytes=64)
            nc.vector.tensor_copy(
                picked[:], scale_table[:].indirect(offsets[:, b * LIST_COLS : (b + 1) * LIST_COLS])
            )
            picked_scales.append(picked)
        for b in range(HALVES):
            dealt = sb.tile([P, D, P], U8, name=f"dealt_scales{b}", align_bytes=64)
            nc.vector.tensor_copy(dealt[:], picked_scales[b][:].rearrange("p (v d) -> p d v", d=D))
            dealt_scales.append(dealt)

        w_grouped = shared.tile([P, M, PACK], BF16, name="w_grouped", offset=WORDS_BYTES // 2, align_bytes=64)
        nc.scalar.activation(w_grouped[:], w_raw[:].rearrange("p t m -> p m t"), ACT.Copy)
        w_words = sb.tile([P, M], U32, name="w_words", align_bytes=64)
        w_scales = sb.tile([P, M], U8, name="w_scales", align_bytes=64)
        nc.vector.quantize_mx(
            out=w_words[:].bitcast(FP8X4),
            scales=w_scales[:],
            in_=w_grouped[:].rearrange("p m t -> p (m t)"),
        )

        mkt_rows = sb.tile([P, M], F32, name="mkt_rows")
        for h in range(ROW_BLOCKS):
            mkt_bank = ps.tile([P, P], F32, name=f"mkt_bank{h}", tag=f"y{h}")
            nc.tensor.transpose(mkt_bank[:], mkt_col[:, h : h + 1].to_broadcast([P, P]), identity[:])
            nc.scalar.activation(mkt_rows[:, h * P : (h + 1) * P], mkt_bank[:], ACT.Copy)

        thr_bias = sb.tile([P, HALVES, D], F32, name="thr_bias")
        nc.scalar.activation(thr_bias[:], thr_col[:], ACT.Copy, scale=0.85)
        half_lgd = sb.tile([P, HALVES, D], F32, name="half_lgd")
        half_sum = sb.tile([P, HALVES], F32, name="half_sum")
        constant = sb.tile([P, HALVES], F32, name="constant")
        for b in range(HALVES):
            nc.scalar.activation(
                half_lgd[:, b, :], lgd_col[:, b, :], ACT.Identity, scale=0.5, accum_out=half_sum[:, b : b + 1]
            )
            nc.scalar.activation(
                constant[:, b : b + 1], att_col[:, b : b + 1], ACT.Identity,
                bias=half_sum[:, b : b + 1], scale=-1.0,
            )

        dealt_words = []
        for b in range(HALVES):
            dealt = shared.tile([P, D, P], U32, name=f"dealt_words{b}", offset=b * WORDS_BYTES, align_bytes=64)
            nc.vector.tensor_copy(
                dealt[:].rearrange("p d v -> p v d"),
                word_table[:].bitcast(U32).indirect(offsets[:, b * LIST_COLS : (b + 1) * LIST_COLS]),
            )
            dealt_words.append(dealt)

        steps = [(b, d) for b in range(HALVES) for d in range(D)]
        PAIR = 2
        tanhs = []
        sums = {}
        for pair in range(len(steps) // PAIR):
            members = steps[PAIR * pair : PAIR * (pair + 1)]
            bank = ps.tile([P, PAIR, M], F32, name=f"y{pair}", tag=f"y{pair}")
            for i, (b, d) in enumerate(members):
                nc.tensor.matmul_mx(
                    out=bank[:, i, :],
                    lhsT=dealt_words[b][:, d, :].bitcast(FP8X4),
                    lhsT_scale=dealt_scales[b][:, d, :],
                    rhs=w_words[:].bitcast(FP8X4),
                    rhs_scale=w_scales[:],
                    start=True,
                    stop=True,
                )
            z = sb.tile([P, PAIR, M], F32, name=f"z{pair}")
            nc.vector.scalar_tensor_tensor(
                z[:], bank[:], -0.7, mkt_rows[:].unsqueeze(1).to_broadcast([P, PAIR, M]), ALU.mult, ALU.add
            )
            for i, (b, d) in enumerate(members):
                t = sb.tile([P, M], F32, name=f"tanh{b}_{d}", tag=f"tanh{b}_{d}")
                nc.scalar.activation(t[:], z[:, i, :], ACT.Tanh, bias=thr_bias[:, b, d : d + 1], scale=0.85)
                tanhs.append(t)

        evens = {}

        def weigh_even(pair):
            b, d = steps[PAIR * pair]
            el = sb.tile([P, M], F32, name=f"even{pair}", tag=f"even{pair}")
            factor = half_lgd[:, b, d : d + 1]
            addend = constant[:, b : b + 1] if d == 0 else 0.0
            if b == 0:
                nc.gpsimd.tensor_scalar(el[:], tanhs[PAIR * pair][:], factor, addend, ALU.mult, ALU.add)
            else:
                nc.scalar.activation(el[:], tanhs[PAIR * pair][:], ACT.Identity, bias=addend, scale=factor)
            evens[pair] = el

        def weigh_odd_and_sum(pair):
            b, d = steps[PAIR * pair + 1]
            el = sb.tile([P, M], F32, name=f"both{pair}")
            nc.vector.scalar_tensor_tensor(
                el[:], tanhs[PAIR * pair + 1][:], half_lgd[:, b, d : d + 1], evens[pair][:], ALU.mult, ALU.add
            )
            for h in range(ROW_BLOCKS):
                if d == 1:
                    sums[(b, h)] = ps.tile([P, P], F32, name=f"sum{b}_{h}", tag=f"sum{b}_{h}")
                nc.tensor.matmul(
                    sums[(b, h)][:], el[:, h * P : (h + 1) * P], identity[:],
                    is_transpose=True, start=(d == 1), stop=(d == D - 1),
                )

        def clamp_and_store(b):
            for h in range(ROW_BLOCKS):
                tag = f"result{h}" if b == 1 else ("tanh1_3", "even3")[h]
                result = sb.tile([P, P], F32, name=f"result{b}_{h}", tag=tag)
                nc.vector.scalar_tensor_tensor(
                    result[:], sums[(b, h)][:], 0.0, wid_rows[:, b * P : (b + 1) * P], ALU.max, ALU.min
                )
                queue = nc.sync if h == 0 else nc.scalar
                queue.dma_start(out[h * P : (h + 1) * P, b * P : (b + 1) * P], result[:])

        weigh_even(0)
        weigh_even(1)
        weigh_even(2)
        weigh_even(3)
        weigh_odd_and_sum(0)
        weigh_odd_and_sum(1)
        weigh_odd_and_sum(2)
        weigh_odd_and_sum(3)
        clamp_and_store(0)
        clamp_and_store(1)
